import numpy as np, ml_dtypes
CORES = [45,53,77,117,47,55,79,119]
N = 8
import mx_ref
NC, W = 128, 4
BF = ml_dtypes.bfloat16
def cut(t, i, w=512):
    return t[:, w * i:w * i + w]
def term(a, B):
    return np.stack([mx_ref.matmul(mx_ref.quantize(cut(a, i)), B) for i in range(4)], axis=2).reshape(128, -1)
def setup_inputs(rng):
    def f(*shape):
        return mx_ref.flush((rng.standard_normal(shape, dtype=np.float32) * np.exp2(rng.integers(-2, 3, shape[:-1] + (1,)))).astype(BF))
    return {"a": f(N, 128, 4 * 512), "b": f(N, 128, 4 * NC)}
def setup_inputs_blocks(rng):
    d = setup_inputs(rng)
    for k in ("a", "b"): d[k] = mx_ref.spread(d[k], rng, 2)
    return d
def setup_inputs_wide(rng):
    d = setup_inputs(rng)
    for k in ("a", "b"): d[k] = mx_ref.flush((d[k].astype(np.float32) * np.exp2(rng.integers(-4, 5, (N, 1, 1))).astype(np.float32)).astype(BF))
    return d
def setup_inputs_lossless(rng):
    a = np.zeros((N, 128, 4 * 128, 4), np.float32)
    for r in range(N):
        k = rng.integers(0, 512, size=4 * 128)
        a[r, k // 4, np.arange(4 * 128), k % 4] = 1.0
    size = np.repeat(2.0 ** rng.integers(-4, 5, size=(1, 1, (4 * NC) // 4)), 4, axis=2)
    b = rng.integers(-1, 2, size=(N, 128, 4 * NC)) * size
    return {"a": a.reshape(N, 128, 4 * 512).astype(BF), "b": b.astype(np.float32).astype(BF)}
def reference(a, b):
    T = [term(a[r], mx_ref.quantize(b[r])) for r in range(N)]
    y = np.zeros((N, 128, 4 * NC), np.float32)
    for c in range(N):
        y[c] = mx_ref.total([T[(c - k) % N] for k in range(W)])
    return {"y": y}

@@ -1,0 +1,178 @@
+from concourse.bass import DstId, RemoteDMATransfer
+from concourse.mybir import dt, AluOpType, ActivationFunctionType
+
+X4 = "float8_e4m3fn_x4"
+SCRATCH = {
+    "abuf": ("sbuf", [128, 2048], "bfloat16"), "bbuf": ("sbuf", [128, 512], "bfloat16"),
+    "acode": ("sbuf", [128, 512], X4), "ascale": ("sbuf", [128, 512], "uint8"),
+    "bcode": ("sbuf", [128, 128], X4), "bscale": ("sbuf", [128, 128], "uint8"),
+    "ones": ("sbuf", [128, 128], "bfloat16"), "ebuf": ("sbuf", [128, 2048], "bfloat16"),
+    "ecode": ("sbuf", [128, 512], X4), "escale": ("sbuf", [128, 512], "uint8"),
+    "tile": ("sbuf", [128, 512], "bfloat16"),
+    "tcode": ("sbuf", [128, 128], X4), "tscale": ("sbuf", [128, 128], "uint8"),
+    "own_c": ("sbuf", [128, 128], X4), "own_s": ("sbuf", [128, 128], "uint8"),
+    "far_c": ("sbuf", [128, 128], X4), "far_s": ("sbuf", [128, 128], "uint8"),
+    "fwd_c": ("sbuf", [128, 128], X4), "fwd_s": ("sbuf", [128, 128], "uint8"),
+    "pair_c": ("sbuf", [128, 128], X4), "pair_s": ("sbuf", [128, 128], "uint8"),
+    "ybuf": ("sbuf", [128, 512], "float32"),
+    "acc": ("psum", [128, 2048], "float32"),
+    "yacc": ("psum", [128, 2048], "float32"),
+}
+SEMAPHORES = (["s_lb", "s_la", "s_la3", "s_stored", "s_zeroed", "s_sel", "s_qe", "s_qb", "s_qt", "s_packed", "s_ycopied",
+               "s_local", "s_own_code", "s_own_scale", "s_far", "s_fwd", "s_pair"]
+              + ["s_qa%d" % i for i in range(4)] + ["s_mm%d" % i for i in range(4)] + ["s_ym%d" % i for i in range(4)])
+
+
+def helpers(T, topo):
+    n, out, taken = len(T.cores), [], []
+    for r in range(n):
+        me = T.cores[r]
+        c = [k for k in range(topo.CHIPS * topo.CORES_PER_CHIP)
+             if topo.chip(k) == topo.chip(me) and k not in T.cores and k not in out
+             and topo.may_write(k, T.cores[(r + 2) % n]) and topo.may_write(k, T.cores[(r + 3) % n])]
+        k = ([x for x in c if (topo.chip(x), topo.die(x)) not in taken] or c)[0]
+        taken.append((topo.chip(k), topo.die(k)))
+        out.append(k)
+    return out
+
+
+def engines(mask):
+    return bin(mask).count("1")
+
+
+def transfer(topo, dst, mask, out, in_, sem):
+    rid, pid, _ = topo.addr(dst)
+    return RemoteDMATransfer(dst_ids=[DstId(rid=rid, pnc=pid)], dma_engine_mask=mask, remote_sem=sem, src=in_, dst=out)
+
+
+def codes(t):
+    return t[:].bitcast(dt.uint8)
+
+
+def bank(acc, b):
+    return acc[:, 512 * b:512 * b + 128]
+
+
+def make_selection(g, T):
+    g.vector.memset(T.ebuf[:], 0.0).then_inc(T.sem.s_zeroed, 1)
+    g.vector.memset(T.ones[:], 1.0).then_inc(T.sem.s_zeroed, 1)
+    g.wait_ge(T.sem.s_zeroed, 2)
+    for b in range(4):
+        g.affine_select(T.ebuf[:, 512 * b + b:512 * b + 512:4], T.ones[:], [[-1, 128]], AluOpType.is_equal, 0.0, 0, 1
+                        ).then_inc(T.sem.s_sel, 1)
+
+
+def quantize_selection(g, T):
+    g.vector.wait_ge(T.sem.s_sel, 4)
+    g.vector.quantize_mx(T.ecode[:], T.escale[:], T.ebuf[:]).then_inc(T.sem.s_qe, 1)
+
+
+def product(g, T, acc, i, start, stop):
+    w = slice(128 * i, 128 * i + 128)
+    return g.tensor.matmul_mx(bank(acc, i), T.acode[:, w], T.ascale[:, w], T.bcode[:], T.bscale[:], start, stop)
+
+
+def unpack(g, T, acc, b, code, scale, start, stop):
+    w = slice(128 * b, 128 * b + 128)
+    return g.tensor.matmul_mx(bank(acc, b), T.ecode[:, w], T.escale[:, w], code[:], scale[:], start, stop)
+
+
+def drain(g, T, acc, out, signals, done):
+    for b in range(4):
+        src, dst = bank(acc, b), out[:, b:512:4]
+        if b % 2 == 0:
+            g.scalar.wait_ge(T.sem[signals % b], 1)
+            g.scalar.activation(dst, src, ActivationFunctionType.Copy).then_inc(T.sem[done], 1)
+        else:
+            g.vector.wait_ge(T.sem[signals % b], 1)
+            g.vector.tensor_copy(dst, src).then_inc(T.sem[done], 1)
+
+
+def quantize_tile(g, T):
+    g.vector.wait_ge(T.sem.s_packed, 4)
+    g.vector.quantize_mx(T.tcode[:], T.tscale[:], T.tile[:]).then_inc(T.sem.s_qt, 1)
+
+
+def rank_core(g, core, r, T, topo):
+    s, n, hs = T.sem, len(T.cores), helpers(T, topo)
+    g.scalar.dma_start(T.bbuf[:], T.b[:]).then_inc(s.s_lb, 16)
+    g.sync.dma_start(T.abuf[:, 0:1536], T.a[:, 0:1536]).then_inc(s.s_la, 16)
+    g.scalar.dma_start(T.abuf[:, 1536:2048], T.a[:, 1536:2048]).then_inc(s.s_la3, 16)
+    make_selection(g, T)
+    g.vector.wait_ge(s.s_lb, 16)
+    g.vector.quantize_mx(T.bcode[:], T.bscale[:], T.bbuf[:]).then_inc(s.s_qb, 1)
+    g.tensor.wait_ge(s.s_qb, 1)
+    for i in range(4):
+        if i == 0:
+            g.vector.wait_ge(s.s_la, 16)
+        if i == 3:
+            g.vector.wait_ge(s.s_la3, 16)
+        w = slice(128 * i, 128 * i + 128)
+        g.vector.quantize_mx(T.acode[:, w], T.ascale[:, w], T.abuf[:, 512 * i:512 * i + 512]).then_inc(s["s_qa%d" % i], 1)
+        g.tensor.wait_ge(s["s_qa%d" % i], 1)
+        product(g, T, T.acc, i, True, True).then_inc(s["s_mm%d" % i], 1)
+    drain(g, T, T.acc, T.tile, "s_mm%d", "s_packed")
+    quantize_tile(g, T)
+    near, far = hs[r], hs[(r - 2) % n]
+    off = topo.mask(core, far)
+    on = topo.mask(core, near) & ~off
+    g.wait_ge(s.s_qt, 1)
+    for out_n, out_f, in_, sem_n in ((codes(T.own_c), codes(T.far_c), codes(T.tcode), s.s_own_code),
+                                     (T.own_s[:], T.far_s[:], T.tscale[:], s.s_own_scale)):
+        g.remote_dma_fused([transfer(topo, far, off, out_f, in_, s.s_far), transfer(topo, near, on, out_n, in_, sem_n)],
+                           local_sem=s.s_local)
+    quantize_selection(g, T)
+    for i in range(4):
+        product(g, T, T.yacc, i, True, False)
+    g.tensor.wait_ge(s.s_qe, 1)
+    g.tensor.wait_ge(s.s_fwd, 2 * engines(topo.mask(hs[(r - 2) % n], core)))
+    for b in range(4):
+        unpack(g, T, T.yacc, b, T.fwd_c, T.fwd_s, False, False)
+    g.tensor.wait_ge(s.s_pair, 2 * engines(topo.mask(hs[(r - 3) % n], core)))
+    for b in range(4):
+        unpack(g, T, T.yacc, b, T.pair_c, T.pair_s, False, True).then_inc(s["s_ym%d" % b], 1)
+    drain(g, T, T.yacc, T.ybuf, "s_ym%d", "s_ycopied")
+    g.sync.wait_ge(s.s_ycopied, 4)
+    g.sync.dma_start(T.y[:], T.ybuf[:]).then_inc(s.s_stored, 16)
+    g.sync.wait_ge(s.s_stored, 16)
+    g.wait_ge(s.s_local, 2 * (engines(off) + engines(on)))
+
+
+def helper_core(g, core, r, T, topo):
+    s, n, hs = T.sem, len(T.cores), helpers(T, topo)
+    make_selection(g, T)
+    quantize_selection(g, T)
+    owner, partner, dest = T.cores[r], T.cores[(r + 2) % n], T.cores[(r + 3) % n]
+    e_own = engines(topo.mask(owner, core) & ~topo.mask(owner, hs[(r - 2) % n]))
+    e_far = engines(topo.mask(partner, core))
+    m_fwd, m_pair = topo.mask(core, partner), topo.mask(core, dest)
+    rid, pid, _ = topo.addr(partner)
+    g.wait_ge(s.s_own_code, e_own)
+    g.remote_dma(codes(T.fwd_c), codes(T.own_c), s.s_fwd, s.s_local, pid, rid, m_fwd)
+    g.wait_ge(s.s_own_scale, e_own)
+    g.remote_dma(T.fwd_s[:], T.own_s[:], s.s_fwd, s.s_local, pid, rid, m_fwd)
+    g.tensor.wait_ge(s.s_qe, 1)
+    g.tensor.wait_ge(s.s_own_code, e_own)
+    g.tensor.wait_ge(s.s_own_scale, e_own)
+    for b in range(4):
+        unpack(g, T, T.acc, b, T.own_c, T.own_s, True, False)
+    g.tensor.wait_ge(s.s_far, 2 * e_far)
+    for b in range(4):
+        unpack(g, T, T.acc, b, T.far_c, T.far_s, False, True).then_inc(s["s_mm%d" % b], 1)
+    drain(g, T, T.acc, T.tile, "s_mm%d", "s_packed")
+    quantize_tile(g, T)
+    rid, pid, _ = topo.addr(dest)
+    g.wait_ge(s.s_qt, 1)
+    g.remote_dma(codes(T.pair_c), codes(T.tcode), s.s_pair, s.s_local, pid, rid, m_pair)
+    g.remote_dma(T.pair_s[:], T.tscale[:], s.s_pair, s.s_local, pid, rid, m_pair)
+    g.wait_ge(s.s_local, 2 * (engines(m_fwd) + engines(m_pair)))
+
+
+def rank_program(g, core, T, topo):
+    r = T.rank_of(core)
+    if r is not None:
+        rank_core(g, core, r, T, topo)
+        return
+    hs = helpers(T, topo)
+    if core in hs:
+        helper_core(g, core, hs.index(core), T, topo)

@@ -2,37 +2,42 @@ from concourse.bass import DstId, RemoteDMATransfer
 from concourse.mybir import dt, AluOpType, ActivationFunctionType
 
 X4 = "float8_e4m3fn_x4"
+HALF = 64
+L4, L5, L3, ZERO, L2, L1, SEL = 0, 64, 128, 192, 320, 384, 448
 SCRATCH = {
     "abuf": ("sbuf", [128, 2048], "bfloat16"), "bbuf": ("sbuf", [128, 512], "bfloat16"),
     "acode": ("sbuf", [128, 512], X4), "ascale": ("sbuf", [128, 512], "uint8"),
     "bcode": ("sbuf", [128, 128], X4), "bscale": ("sbuf", [128, 128], "uint8"),
-    "ones": ("sbuf", [128, 128], "bfloat16"), "ebuf": ("sbuf", [128, 2048], "bfloat16"),
-    "ecode": ("sbuf", [128, 512], X4), "escale": ("sbuf", [128, 512], "uint8"),
-    "tile": ("sbuf", [128, 512], "bfloat16"),
-    "tcode": ("sbuf", [128, 128], X4), "tscale": ("sbuf", [128, 128], "uint8"),
-    "own_c": ("sbuf", [128, 128], X4), "own_s": ("sbuf", [128, 128], "uint8"),
-    "far_c": ("sbuf", [128, 128], X4), "far_s": ("sbuf", [128, 128], "uint8"),
-    "fwd_c": ("sbuf", [128, 128], X4), "fwd_s": ("sbuf", [128, 128], "uint8"),
-    "pair_c": ("sbuf", [128, 128], X4), "pair_s": ("sbuf", [128, 128], "uint8"),
-    "ybuf": ("sbuf", [128, 512], "float32"),
-    "acc": ("psum", [128, 2048], "float32"),
-    "yacc": ("psum", [128, 2048], "float32"),
+    "ones": ("sbuf", [128, 128], "bfloat16"), "ebuf": ("sbuf", [128, 516], "bfloat16"),
+    "wc": ("sbuf", [128, 960], X4), "ws": ("sbuf", [128, 960], "uint8"),
+    "t0": ("sbuf", [128, 512], "bfloat16"), "t1": ("sbuf", [128, 768], "bfloat16"),
+    "tq": ("sbuf", [128, 512], "bfloat16"),
+    "t0c": ("sbuf", [128, 128], X4), "t0s": ("sbuf", [128, 128], "uint8"),
+    "t1c": ("sbuf", [128, 128], X4), "t1s": ("sbuf", [128, 128], "uint8"),
+    "tqc": ("sbuf", [128, 128], X4), "tqs": ("sbuf", [128, 128], "uint8"),
+    "ytmp": ("sbuf", [128, 256], "float32"), "ybuf": ("sbuf", [128, 512], "float32"),
+    "acc": ("psum", [128, 4096], "float32"),
 }
-SEMAPHORES = (["s_lb", "s_la", "s_la3", "s_stored", "s_zeroed", "s_sel", "s_qe", "s_qb", "s_qt", "s_packed", "s_ycopied",
-               "s_local", "s_own_code", "s_own_scale", "s_far", "s_fwd", "s_pair"]
-              + ["s_qa%d" % i for i in range(4)] + ["s_mm%d" % i for i in range(4)] + ["s_ym%d" % i for i in range(4)])
+SEMAPHORES = (["s_lb", "s_la0", "s_la1", "s_stored", "s_zeroed", "s_pad", "s_padq", "s_sel", "s_qe", "s_qz", "s_qb", "s_pk0",
+               "s_pk1", "s_pkq", "s_qt0", "s_qt1", "s_qtq", "s_yc0", "s_yh0", "s_yh1", "s_local", "s_own", "s_fc", "s_fs",
+               "s_rc", "s_rs", "s_fwd", "s_pair", "s_d1", "s_d2", "s_d3"]
+              + ["s_%s%d" % (k, i) for k in ("qa", "mm", "yq", "ya", "yb", "cp") for i in range(4)])
 
 
-def helpers(T, topo):
-    n, out, taken = len(T.cores), [], []
+def plan(T, topo):
+    n, out, taken = len(T.cores), {}, []
+
+    def free(k, r):
+        return topo.may_write(k, T.cores[(r + 1) % n]) and topo.may_write(k, T.cores[(r + 3) % n])
     for r in range(n):
-        me = T.cores[r]
-        c = [k for k in range(topo.CHIPS * topo.CORES_PER_CHIP)
-             if topo.chip(k) == topo.chip(me) and k not in T.cores and k not in out
-             and topo.may_write(k, T.cores[(r + 2) % n]) and topo.may_write(k, T.cores[(r + 3) % n])]
-        k = ([x for x in c if (topo.chip(x), topo.die(x)) not in taken] or c)[0]
-        taken.append((topo.chip(k), topo.die(k)))
-        out.append(k)
+        own = T.cores[r]
+        out[r] = {}
+        for job, same_die in ([(2, False)] if free(own, r) else [(1, True), (3, False), (0, False)]):
+            c = [k for k in range(topo.CHIPS * topo.CORES_PER_CHIP) if topo.chip(k) == topo.chip(own)
+                 and k not in T.cores and k not in taken and free(k, r) == (job != 2)]
+            k = ([x for x in c if (topo.die(x) == topo.die(own)) == same_die] or c)[0]
+            taken.append(k)
+            out[r][job] = k
     return out
 
 
@@ -40,132 +45,263 @@ def engines(mask):
     return bin(mask).count("1")
 
 
-def transfer(topo, dst, mask, out, in_, sem):
+def halves(mask):
+    e = [k for k in range(mask.bit_length()) if mask >> k & 1]
+    return [sum(1 << k for k in part) for part in (e[:len(e) // 2], e[len(e) // 2:])]
+
+
+def maker(T, hs, c):
+    return hs[c].get(0, T.cores[c])
+
+
+def off_mask(T, topo, r):
+    return topo.mask(T.cores[r], T.cores[(r + 2) % len(T.cores)])
+
+
+def on_mask(T, topo, hs, r):
+    return topo.mask(T.cores[r], list(hs[r].values())[0]) & ~off_mask(T, topo, r)
+
+
+def crossing(T, topo, hs, r, d):
+    dst = T.cores[(r + d) % len(T.cores)]
+    if d in hs[r]:
+        return hs[r][d], topo.mask(hs[r][d], dst)
+    off = topo.mask(T.cores[r], dst)
+    return T.cores[r], off if d == 2 else halves(off)[0 if d == 1 else 1]
+
+
+def order(hs, c):
+    return sorted((2, 1, 3), key=lambda d: d in hs[(c - d) % len(hs)])
+
+
+def slot(hs, c, d):
+    return (L3, L4, L5)[order(hs, c).index(d)]
+
+
+def fused(g, topo, transfers, local):
+    calls = []
+    for dst, mask, out, in_, sem in transfers:
+        rid, pid, _ = topo.addr(dst)
+        calls.append(RemoteDMATransfer(dst_ids=[DstId(rid=rid, pnc=pid)], dma_engine_mask=mask, remote_sem=sem, src=in_, dst=out))
+    g.remote_dma_fused(calls, local_sem=local)
+    return sum(engines(t[1]) for t in transfers)
+
+
+def send(g, topo, dst, mask, out, in_, sem, local):
     rid, pid, _ = topo.addr(dst)
-    return RemoteDMATransfer(dst_ids=[DstId(rid=rid, pnc=pid)], dma_engine_mask=mask, remote_sem=sem, src=in_, dst=out)
+    g.remote_dma(out, in_, sem, local, pid, rid, mask)
+    return engines(mask)
 
 
-def codes(t):
-    return t[:].bitcast(dt.uint8)
+def half_c(t, a):
+    return t[:, a:a + HALF].bitcast(dt.uint8)
 
 
-def bank(acc, b):
-    return acc[:, 512 * b:512 * b + 128]
+def half_s(t, a):
+    return t[:, a:a + HALF]
+
+
+def sums(acc, k, n=HALF, at=0):
+    return acc[:, 512 * k + at:512 * k + at + n]
 
 
 def make_selection(g, T):
     g.vector.memset(T.ebuf[:], 0.0).then_inc(T.sem.s_zeroed, 1)
     g.vector.memset(T.ones[:], 1.0).then_inc(T.sem.s_zeroed, 1)
     g.wait_ge(T.sem.s_zeroed, 2)
-    for b in range(4):
-        g.affine_select(T.ebuf[:, 512 * b + b:512 * b + 512:4], T.ones[:], [[-1, 128]], AluOpType.is_equal, 0.0, 0, 1
-                        ).then_inc(T.sem.s_sel, 1)
+    g.affine_select(T.ebuf[:, 3:515:4], T.ones[:], [[-1, 128]], AluOpType.is_equal, 0.0, 0, 1).then_inc(T.sem.s_sel, 1)
 
 
 def quantize_selection(g, T):
-    g.vector.wait_ge(T.sem.s_sel, 4)
-    g.vector.quantize_mx(T.ecode[:], T.escale[:], T.ebuf[:]).then_inc(T.sem.s_qe, 1)
+    g.vector.wait_ge(T.sem.s_sel, 1)
+    for t in range(4):
+        w = slice(SEL + 128 * t, SEL + 128 * t + 128)
+        g.vector.quantize_mx(T.wc[:, w], T.ws[:, w], T.ebuf[:, 3 - t:515 - t]).then_inc(T.sem.s_qe, 1)
 
 
-def product(g, T, acc, i, start, stop):
-    w = slice(128 * i, 128 * i + 128)
-    return g.tensor.matmul_mx(bank(acc, i), T.acode[:, w], T.ascale[:, w], T.bcode[:], T.bscale[:], start, stop)
+def unpack(g, T, first_bank, codes, scales, at, start, stop, signals=None):
+    m = slice(at, at + 128)
+    for t in range(4):
+        w = slice(SEL + 128 * t, SEL + 128 * t + 128)
+        call = g.tensor.matmul_mx(sums(T.acc, first_bank + t, 128), T.wc[:, w], T.ws[:, w], codes[:, m], scales[:, m], start, stop)
+        if signals:
+            call.then_inc(T.sem[signals % t], 1)
 
 
-def unpack(g, T, acc, b, code, scale, start, stop):
-    w = slice(128 * b, 128 * b + 128)
-    return g.tensor.matmul_mx(bank(acc, b), T.ecode[:, w], T.escale[:, w], code[:], scale[:], start, stop)
-
-
-def drain(g, T, acc, out, signals, done):
-    for b in range(4):
-        src, dst = bank(acc, b), out[:, b:512:4]
-        if b % 2 == 0:
-            g.scalar.wait_ge(T.sem[signals % b], 1)
+def drain_sums(g, T, signals, out, first, done):
+    for t in range(4):
+        a = first(t // 2, t % 2)
+        dst, src = out[:, a:a + 4 * (HALF - 1) + 1:4], sums(T.acc, t)
+        if t % 2 == 0:
+            g.scalar.wait_ge(T.sem[signals % t], 1)
             g.scalar.activation(dst, src, ActivationFunctionType.Copy).then_inc(T.sem[done], 1)
         else:
-            g.vector.wait_ge(T.sem[signals % b], 1)
+            g.vector.wait_ge(T.sem[signals % t], 1)
             g.vector.tensor_copy(dst, src).then_inc(T.sem[done], 1)
 
 
-def quantize_tile(g, T):
-    g.vector.wait_ge(T.sem.s_packed, 4)
-    g.vector.quantize_mx(T.tcode[:], T.tscale[:], T.tile[:]).then_inc(T.sem.s_qt, 1)
-
-
-def rank_core(g, core, r, T, topo):
-    s, n, hs = T.sem, len(T.cores), helpers(T, topo)
-    g.scalar.dma_start(T.bbuf[:], T.b[:]).then_inc(s.s_lb, 16)
-    g.sync.dma_start(T.abuf[:, 0:1536], T.a[:, 0:1536]).then_inc(s.s_la, 16)
-    g.scalar.dma_start(T.abuf[:, 1536:2048], T.a[:, 1536:2048]).then_inc(s.s_la3, 16)
-    make_selection(g, T)
-    g.vector.wait_ge(s.s_lb, 16)
-    g.vector.quantize_mx(T.bcode[:], T.bscale[:], T.bbuf[:]).then_inc(s.s_qb, 1)
-    g.tensor.wait_ge(s.s_qb, 1)
-    for i in range(4):
-        if i == 0:
-            g.vector.wait_ge(s.s_la, 16)
-        if i == 3:
-            g.vector.wait_ge(s.s_la3, 16)
+def term_chunk(g, T, k):
+    s, tile, done = T.sem, (T.t0, T.t1)[k], ("s_pk0", "s_pk1")[k]
+    g.vector.wait_ge(s["s_la%d" % k], 16)
+    for i in (2 * k, 2 * k + 1):
         w = slice(128 * i, 128 * i + 128)
         g.vector.quantize_mx(T.acode[:, w], T.ascale[:, w], T.abuf[:, 512 * i:512 * i + 512]).then_inc(s["s_qa%d" % i], 1)
         g.tensor.wait_ge(s["s_qa%d" % i], 1)
-        product(g, T, T.acc, i, True, True).then_inc(s["s_mm%d" % i], 1)
-    drain(g, T, T.acc, T.tile, "s_mm%d", "s_packed")
-    quantize_tile(g, T)
-    near, far = hs[r], hs[(r - 2) % n]
-    off = topo.mask(core, far)
-    on = topo.mask(core, near) & ~off
-    g.wait_ge(s.s_qt, 1)
-    for out_n, out_f, in_, sem_n in ((codes(T.own_c), codes(T.far_c), codes(T.tcode), s.s_own_code),
-                                     (T.own_s[:], T.far_s[:], T.tscale[:], s.s_own_scale)):
-        g.remote_dma_fused([transfer(topo, far, off, out_f, in_, s.s_far), transfer(topo, near, on, out_n, in_, sem_n)],
-                           local_sem=s.s_local)
+        g.tensor.matmul_mx(sums(T.acc, 4 + i, 128), T.acode[:, w], T.ascale[:, w], T.bcode[:], T.bscale[:], True, True
+                           ).then_inc(s["s_mm%d" % i], 1)
+    g.scalar.wait_ge(s["s_mm%d" % (2 * k)], 1)
+    g.vector.wait_ge(s["s_mm%d" % (2 * k + 1)], 1)
+    for h in range(2):
+        g.scalar.activation(tile[:, 2 * h:256:4], sums(T.acc, 4 + 2 * k, HALF, HALF * h), ActivationFunctionType.Copy
+                            ).then_inc(s[done], 1)
+        g.vector.tensor_copy(tile[:, 2 * h + 1:256:4], sums(T.acc, 5 + 2 * k, HALF, HALF * h)).then_inc(s[done], 1)
+    g.vector.wait_ge(s[done], 4)
+    code, scale = ((T.t0c, T.t0s), (T.t1c, T.t1s))[k]
+    g.vector.quantize_mx(code[:], scale[:], tile[:, 0:512]).then_inc(s["s_qt%d" % k], 1)
+
+
+def make_q(g, T):
+    s = T.sem
+    drain_sums(g, T, "s_yq%d", T.tq, lambda h, i: 2 * h + i, "s_pkq")
+    g.vector.wait_ge(s.s_padq, 1)
+    g.vector.wait_ge(s.s_pkq, 4)
+    g.vector.quantize_mx(T.tqc[:], T.tqs[:], T.tq[:]).then_inc(s.s_qtq, 1)
+
+
+def send_q(g, T, topo, core, c):
+    s, dst = T.sem, T.cores[(c + 1) % len(T.cores)]
+    m = topo.mask(core, dst)
+    g.wait_ge(s.s_qtq, 1)
+    return (send(g, topo, dst, m, half_c(T.wc, L2), half_c(T.tqc, 0), s.s_pair, s.s_local)
+            + send(g, topo, dst, m, half_s(T.ws, L2), half_s(T.tqs, 0), s.s_pair, s.s_local))
+
+
+def rank_core(g, core, r, T, topo):
+    s, n = T.sem, len(T.cores)
+    hs = plan(T, topo)
+    free = 0 not in hs[r]
+    g.scalar.dma_start(T.bbuf[:], T.b[:]).then_inc(s.s_lb, 16)
+    g.sync.dma_start(T.abuf[:, 0:1024], T.a[:, 0:1024]).then_inc(s.s_la0, 16)
+    g.scalar.dma_start(T.abuf[:, 1024:2048], T.a[:, 1024:2048]).then_inc(s.s_la1, 16)
+    make_selection(g, T)
+    g.vector.memset(T.t0[:, 256:512], 0.0).then_inc(s.s_pad, 1)
+    g.vector.memset(T.t1[:, 256:768], 0.0).then_inc(s.s_pad, 1)
+    if free:
+        g.vector.memset(T.tq[:, 256:512], 0.0).then_inc(s.s_padq, 1)
+    g.vector.wait_ge(s.s_pad, 2)
+    g.vector.quantize_mx(T.wc[:, ZERO:ZERO + 128], T.ws[:, ZERO:ZERO + 128], T.t1[:, 256:768]).then_inc(s.s_qz, 1)
+    g.vector.wait_ge(s.s_lb, 16)
+    g.vector.quantize_mx(T.bcode[:], T.bscale[:], T.bbuf[:]).then_inc(s.s_qb, 1)
+    g.tensor.wait_ge(s.s_qb, 1)
+    term_chunk(g, T, 0)
+    term_chunk(g, T, 1)
     quantize_selection(g, T)
-    for i in range(4):
-        product(g, T, T.yacc, i, True, False)
-    g.tensor.wait_ge(s.s_qe, 1)
-    g.tensor.wait_ge(s.s_fwd, 2 * engines(topo.mask(hs[(r - 2) % n], core)))
-    for b in range(4):
-        unpack(g, T, T.yacc, b, T.fwd_c, T.fwd_s, False, False)
-    g.tensor.wait_ge(s.s_pair, 2 * engines(topo.mask(hs[(r - 3) % n], core)))
-    for b in range(4):
-        unpack(g, T, T.yacc, b, T.pair_c, T.pair_s, False, True).then_inc(s["s_ym%d" % b], 1)
-    drain(g, T, T.yacc, T.ybuf, "s_ym%d", "s_ycopied")
-    g.sync.wait_ge(s.s_ycopied, 4)
-    g.sync.dma_start(T.y[:], T.ybuf[:]).then_inc(s.s_stored, 16)
-    g.sync.wait_ge(s.s_stored, 16)
-    g.wait_ge(s.s_local, 2 * (engines(off) + engines(on)))
+    to2, q2 = T.cores[(r + 2) % n], maker(T, hs, (r + 2) % n)
+    off, on = off_mask(T, topo, r), on_mask(T, topo, hs, r)
+    code, scale = half_c(T.t0c, 0), half_s(T.t0s, 0)
+    at, sem_c, sem_s = (L1, s.s_fwd, s.s_fwd) if q2 == to2 else (L2, s.s_fc, s.s_fs)
+    out_c, out_s = [(q2, off, half_c(T.wc, at), code, sem_c)], [(q2, off, half_s(T.ws, at), scale, sem_s)]
+    if not free:
+        out_c.append((hs[r][0], on, half_c(T.wc, L1), code, s.s_own))
+        out_s.append((hs[r][0], on, half_s(T.ws, L1), scale, s.s_own))
+    g.wait_ge(s.s_qt0, 1)
+    sent = fused(g, topo, out_c, s.s_local)
+    sent += fused(g, topo, out_s, s.s_local)
+    to = []
+    for d in (1, 2, 3):
+        if d in hs[r]:
+            to.append((hs[r][d], off if d == 1 else on, L3, s.s_rc, s.s_rs))
+        elif free:
+            c = (r + d) % n
+            to.append((T.cores[c], crossing(T, topo, hs, r, d)[1], slot(hs, c, d), s["s_d%d" % d], s["s_d%d" % d]))
+    g.wait_ge(s.s_qt1, 1)
+    sent += fused(g, topo, [(k, m, half_c(T.wc, a), half_c(T.t1c, 0), sc) for k, m, a, sc, ss in to], s.s_local)
+    sent += fused(g, topo, [(k, m, half_s(T.ws, a), half_s(T.t1s, 0), ss) for k, m, a, sc, ss in to], s.s_local)
+    if not free:
+        a = slot(hs, (r + 2) % n, 2)
+        sent += send(g, topo, to2, off, half_c(T.wc, a), half_c(T.t1c, 0), s.s_d2, s.s_local)
+        sent += send(g, topo, to2, off, half_s(T.ws, a), half_s(T.t1s, 0), s.s_d2, s.s_local)
+    if q2 != to2:
+        sent += send(g, topo, to2, off, half_s(T.ws, L1), scale, s.s_fwd, s.s_local)
+    e_far = engines(off_mask(T, topo, (r - 2) % n))
+    e_fwd = e_far + (e_far if free else engines(topo.mask(hs[r][0], core) & topo.mask(hs[r][0], T.cores[(r + 1) % n])))
+
+    def wait_term(d):
+        g.tensor.wait_ge(s["s_d%d" % d], 2 * engines(crossing(T, topo, hs, (r - d) % n, d)[1]))
+    first, second, third = order(hs, r)
+    g.tensor.wait_ge(s.s_qe, 4)
+    g.tensor.wait_ge(s.s_qt0, 1)
+    unpack(g, T, 0, T.t0c, T.t0s, 0, True, False)
+    g.tensor.wait_ge(s.s_qt1, 1)
+    unpack(g, T, 4, T.t1c, T.t1s, 0, True, False)
+    g.tensor.wait_ge(s.s_qz, 1)
+    if free:
+        g.tensor.wait_ge(s.s_fwd, e_fwd)
+        unpack(g, T, 0, T.wc, T.ws, L1, False, True, "s_yq%d")
+        make_q(g, T)
+        sent += send_q(g, T, topo, core, r)
+        g.tensor.wait_ge(s.s_qtq, 1)
+        unpack(g, T, 0, T.t0c, T.t0s, 0, True, False)
+        unpack(g, T, 0, T.wc, T.ws, L1, False, False)
+        wait_term(first)
+        unpack(g, T, 4, T.wc, T.ws, L3, False, False)
+    else:
+        wait_term(first)
+        unpack(g, T, 4, T.wc, T.ws, L3, False, False)
+        g.tensor.wait_ge(s.s_fwd, e_fwd)
+        unpack(g, T, 0, T.wc, T.ws, L1, False, False)
+    g.tensor.wait_ge(s.s_pair, 2 * engines(topo.mask(maker(T, hs, (r - 1) % n), core)))
+    unpack(g, T, 0, T.wc, T.ws, L2, False, True, "s_ya%d")
+    wait_term(second)
+    wait_term(third)
+    unpack(g, T, 4, T.wc, T.ws, L4, False, True, "s_yb%d")
+    drain_sums(g, T, "s_ya%d", T.ybuf, lambda h, i: 256 * h + i, "s_yc0")
+    for t in range(4):
+        h, i = t // 2, t % 2
+        tmp = T.ytmp[:, HALF * t:HALF * t + HALF]
+        g.scalar.wait_ge(s["s_yb%d" % t], 1)
+        g.scalar.activation(tmp, sums(T.acc, 4 + t, HALF, HALF), ActivationFunctionType.Copy).then_inc(s["s_cp%d" % t], 1)
+        g.vector.wait_ge(s["s_cp%d" % t], 1)
+        g.vector.tensor_tensor(T.ybuf[:, 256 * h + 2 + i:256 * h + 256:4], sums(T.acc, 4 + t), tmp, AluOpType.add
+                               ).then_inc(s["s_yh%d" % h], 1)
+    for h, queue in ((0, g.sync), (1, g.scalar)):
+        queue.wait_ge(s.s_yc0, 4)
+        queue.wait_ge(s["s_yh%d" % h], 2)
+        queue.dma_start(T.y[:, 256 * h:256 * h + 256], T.ybuf[:, 256 * h:256 * h + 256]).then_inc(s.s_stored, 16)
+    g.sync.wait_ge(s.s_stored, 32)
+    g.wait_ge(s.s_local, sent)
 
 
-def helper_core(g, core, r, T, topo):
-    s, n, hs = T.sem, len(T.cores), helpers(T, topo)
+def q_helper(g, core, r, hs, T, topo):
+    s, n = T.sem, len(T.cores)
+    owner = T.cores[r]
     make_selection(g, T)
     quantize_selection(g, T)
-    owner, partner, dest = T.cores[r], T.cores[(r + 2) % n], T.cores[(r + 3) % n]
-    e_own = engines(topo.mask(owner, core) & ~topo.mask(owner, hs[(r - 2) % n]))
-    e_far = engines(topo.mask(partner, core))
-    m_fwd, m_pair = topo.mask(core, partner), topo.mask(core, dest)
-    rid, pid, _ = topo.addr(partner)
-    g.wait_ge(s.s_own_code, e_own)
-    g.remote_dma(codes(T.fwd_c), codes(T.own_c), s.s_fwd, s.s_local, pid, rid, m_fwd)
-    g.wait_ge(s.s_own_scale, e_own)
-    g.remote_dma(T.fwd_s[:], T.own_s[:], s.s_fwd, s.s_local, pid, rid, m_fwd)
-    g.tensor.wait_ge(s.s_qe, 1)
-    g.tensor.wait_ge(s.s_own_code, e_own)
-    g.tensor.wait_ge(s.s_own_scale, e_own)
-    for b in range(4):
-        unpack(g, T, T.acc, b, T.own_c, T.own_s, True, False)
-    g.tensor.wait_ge(s.s_far, 2 * e_far)
-    for b in range(4):
-        unpack(g, T, T.acc, b, T.far_c, T.far_s, False, True).then_inc(s["s_mm%d" % b], 1)
-    drain(g, T, T.acc, T.tile, "s_mm%d", "s_packed")
-    quantize_tile(g, T)
-    rid, pid, _ = topo.addr(dest)
-    g.wait_ge(s.s_qt, 1)
-    g.remote_dma(codes(T.pair_c), codes(T.tcode), s.s_pair, s.s_local, pid, rid, m_pair)
-    g.remote_dma(T.pair_s[:], T.tscale[:], s.s_pair, s.s_local, pid, rid, m_pair)
-    g.wait_ge(s.s_local, 2 * (engines(m_fwd) + engines(m_pair)))
+    g.vector.memset(T.tq[:, 256:512], 0.0).then_inc(s.s_padq, 1)
+    e_far, e_own = engines(off_mask(T, topo, (r - 2) % n)), engines(on_mask(T, topo, hs, r))
+    m = topo.mask(core, owner) & topo.mask(core, T.cores[(r + 1) % n])
+    g.wait_ge(s.s_fc, e_far)
+    sent = send(g, topo, owner, m, half_c(T.wc, L1), half_c(T.wc, L2), s.s_fwd, s.s_local)
+    g.tensor.wait_ge(s.s_qe, 4)
+    g.tensor.wait_ge(s.s_own, 2 * e_own)
+    unpack(g, T, 0, T.wc, T.ws, L1, True, False)
+    g.tensor.wait_ge(s.s_fc, e_far)
+    g.tensor.wait_ge(s.s_fs, e_far)
+    unpack(g, T, 0, T.wc, T.ws, L2, False, True, "s_yq%d")
+    make_q(g, T)
+    sent += send_q(g, T, topo, core, r)
+    g.wait_ge(s.s_local, sent)
+
+
+def relay(g, core, r, d, hs, T, topo):
+    s, c = T.sem, (r + d) % len(T.cores)
+    dst, a, sem = T.cores[c], slot(hs, c, d), s["s_d%d" % d]
+    m, came = topo.mask(core, dst), engines(off_mask(T, topo, r) if d == 1 else on_mask(T, topo, hs, r))
+    g.wait_ge(s.s_rc, came)
+    sent = send(g, topo, dst, m, half_c(T.wc, a), half_c(T.wc, L3), sem, s.s_local)
+    g.wait_ge(s.s_rs, came)
+    sent += send(g, topo, dst, m, half_s(T.ws, a), half_s(T.ws, L3), sem, s.s_local)
+    g.wait_ge(s.s_local, sent)
 
 
 def rank_program(g, core, T, topo):
@@ -173,6 +309,10 @@ def rank_program(g, core, T, topo):
     if r is not None:
         rank_core(g, core, r, T, topo)
         return
-    hs = helpers(T, topo)
-    if core in hs:
-        helper_core(g, core, hs.index(core), T, topo)
+    hs = plan(T, topo)
+    for k in range(len(T.cores)):
+        for job, helper in hs[k].items():
+            if helper == core and job == 0:
+                q_helper(g, core, k, hs, T, topo)
+            elif helper == core:
+                relay(g, core, k, job, hs, T, topo)

from concourse.bass import DstId, RemoteDMATransfer
from concourse.mybir import dt, AluOpType, ActivationFunctionType

X4 = "float8_e4m3fn_x4"
HALF = 64
L4, L5, L3, ZERO, L2, L1, SEL = 0, 64, 128, 192, 320, 384, 448
SCRATCH = {
    "abuf": ("sbuf", [128, 2048], "bfloat16"), "bbuf": ("sbuf", [128, 512], "bfloat16"),
    "acode": ("sbuf", [128, 512], X4), "ascale": ("sbuf", [128, 512], "uint8"),
    "bcode": ("sbuf", [128, 128], X4), "bscale": ("sbuf", [128, 128], "uint8"),
    "ones": ("sbuf", [128, 128], "bfloat16"), "ebuf": ("sbuf", [128, 516], "bfloat16"),
    "wc": ("sbuf", [128, 960], X4), "ws": ("sbuf", [128, 960], "uint8"),
    "t0": ("sbuf", [128, 512], "bfloat16"), "t1": ("sbuf", [128, 768], "bfloat16"),
    "tq": ("sbuf", [128, 512], "bfloat16"),
    "t0c": ("sbuf", [128, 128], X4), "t0s": ("sbuf", [128, 128], "uint8"),
    "t1c": ("sbuf", [128, 128], X4), "t1s": ("sbuf", [128, 128], "uint8"),
    "tqc": ("sbuf", [128, 128], X4), "tqs": ("sbuf", [128, 128], "uint8"),
    "ytmp": ("sbuf", [128, 256], "float32"), "ybuf": ("sbuf", [128, 512], "float32"),
    "acc": ("psum", [128, 4096], "float32"),
}
SEMAPHORES = (["s_lb", "s_la0", "s_la1", "s_stored", "s_zeroed", "s_pad", "s_padq", "s_sel", "s_qe", "s_qz", "s_qb", "s_pk0",
               "s_pk1", "s_pkq", "s_qt0", "s_qt1", "s_qtq", "s_yc0", "s_yh0", "s_yh1", "s_local", "s_own", "s_fc", "s_fs",
               "s_rc", "s_rs", "s_fwd", "s_pair", "s_d1", "s_d2", "s_d3"]
              + ["s_%s%d" % (k, i) for k in ("qa", "mm", "yq", "ya", "yb", "cp") for i in range(4)])


def plan(T, topo):
    n, out, taken = len(T.cores), {}, []

    def free(k, r):
        return topo.may_write(k, T.cores[(r + 1) % n]) and topo.may_write(k, T.cores[(r + 3) % n])
    for r in range(n):
        own = T.cores[r]
        out[r] = {}
        for job, same_die in ([(2, False)] if free(own, r) else [(1, True), (3, False), (0, False)]):
            c = [k for k in range(topo.CHIPS * topo.CORES_PER_CHIP) if topo.chip(k) == topo.chip(own)
                 and k not in T.cores and k not in taken and free(k, r) == (job != 2)]
            k = ([x for x in c if (topo.die(x) == topo.die(own)) == same_die] or c)[0]
            taken.append(k)
            out[r][job] = k
    return out


def engines(mask):
    return bin(mask).count("1")


def halves(mask):
    e = [k for k in range(mask.bit_length()) if mask >> k & 1]
    return [sum(1 << k for k in part) for part in (e[:len(e) // 2], e[len(e) // 2:])]


def maker(T, hs, c):
    return hs[c].get(0, T.cores[c])


def off_mask(T, topo, r):
    return topo.mask(T.cores[r], T.cores[(r + 2) % len(T.cores)])


def on_mask(T, topo, hs, r):
    return topo.mask(T.cores[r], list(hs[r].values())[0]) & ~off_mask(T, topo, r)


def crossing(T, topo, hs, r, d):
    dst = T.cores[(r + d) % len(T.cores)]
    if d in hs[r]:
        return hs[r][d], topo.mask(hs[r][d], dst)
    off = topo.mask(T.cores[r], dst)
    return T.cores[r], off if d == 2 else halves(off)[0 if d == 1 else 1]


def order(hs, c):
    return sorted((2, 1, 3), key=lambda d: d in hs[(c - d) % len(hs)])


def slot(hs, c, d):
    return (L3, L4, L5)[order(hs, c).index(d)]


def fused(g, topo, transfers, local):
    calls = []
    for dst, mask, out, in_, sem in transfers:
        rid, pid, _ = topo.addr(dst)
        calls.append(RemoteDMATransfer(dst_ids=[DstId(rid=rid, pnc=pid)], dma_engine_mask=mask, remote_sem=sem, src=in_, dst=out))
    g.remote_dma_fused(calls, local_sem=local)
    return sum(engines(t[1]) for t in transfers)


def send(g, topo, dst, mask, out, in_, sem, local):
    rid, pid, _ = topo.addr(dst)
    g.remote_dma(out, in_, sem, local, pid, rid, mask)
    return engines(mask)


def half_c(t, a):
    return t[:, a:a + HALF].bitcast(dt.uint8)


def half_s(t, a):
    return t[:, a:a + HALF]


def sums(acc, k, n=HALF, at=0):
    return acc[:, 512 * k + at:512 * k + at + n]


def make_selection(g, T):
    g.vector.memset(T.ebuf[:], 0.0).then_inc(T.sem.s_zeroed, 1)
    g.vector.memset(T.ones[:], 1.0).then_inc(T.sem.s_zeroed, 1)
    g.wait_ge(T.sem.s_zeroed, 2)
    g.affine_select(T.ebuf[:, 3:515:4], T.ones[:], [[-1, 128]], AluOpType.is_equal, 0.0, 0, 1).then_inc(T.sem.s_sel, 1)


def quantize_selection(g, T):
    g.vector.wait_ge(T.sem.s_sel, 1)
    for t in range(4):
        w = slice(SEL + 128 * t, SEL + 128 * t + 128)
        g.vector.quantize_mx(T.wc[:, w], T.ws[:, w], T.ebuf[:, 3 - t:515 - t]).then_inc(T.sem.s_qe, 1)


def unpack(g, T, first_bank, codes, scales, at, start, stop, signals=None):
    m = slice(at, at + 128)
    for t in range(4):
        w = slice(SEL + 128 * t, SEL + 128 * t + 128)
        call = g.tensor.matmul_mx(sums(T.acc, first_bank + t, 128), T.wc[:, w], T.ws[:, w], codes[:, m], scales[:, m], start, stop)
        if signals:
            call.then_inc(T.sem[signals % t], 1)


def drain_sums(g, T, signals, out, first, done):
    for t in range(4):
        a = first(t // 2, t % 2)
        dst, src = out[:, a:a + 4 * (HALF - 1) + 1:4], sums(T.acc, t)
        if t % 2 == 0:
            g.scalar.wait_ge(T.sem[signals % t], 1)
            g.scalar.activation(dst, src, ActivationFunctionType.Copy).then_inc(T.sem[done], 1)
        else:
            g.vector.wait_ge(T.sem[signals % t], 1)
            g.vector.tensor_copy(dst, src).then_inc(T.sem[done], 1)


def term_chunk(g, T, k):
    s, tile, done = T.sem, (T.t0, T.t1)[k], ("s_pk0", "s_pk1")[k]
    g.vector.wait_ge(s["s_la%d" % k], 16)
    for i in (2 * k, 2 * k + 1):
        w = slice(128 * i, 128 * i + 128)
        g.vector.quantize_mx(T.acode[:, w], T.ascale[:, w], T.abuf[:, 512 * i:512 * i + 512]).then_inc(s["s_qa%d" % i], 1)
        g.tensor.wait_ge(s["s_qa%d" % i], 1)
        g.tensor.matmul_mx(sums(T.acc, 4 + i, 128), T.acode[:, w], T.ascale[:, w], T.bcode[:], T.bscale[:], True, True
                           ).then_inc(s["s_mm%d" % i], 1)
    g.scalar.wait_ge(s["s_mm%d" % (2 * k)], 1)
    g.vector.wait_ge(s["s_mm%d" % (2 * k + 1)], 1)
    for h in range(2):
        g.scalar.activation(tile[:, 2 * h:256:4], sums(T.acc, 4 + 2 * k, HALF, HALF * h), ActivationFunctionType.Copy
                            ).then_inc(s[done], 1)
        g.vector.tensor_copy(tile[:, 2 * h + 1:256:4], sums(T.acc, 5 + 2 * k, HALF, HALF * h)).then_inc(s[done], 1)
    g.vector.wait_ge(s[done], 4)
    code, scale = ((T.t0c, T.t0s), (T.t1c, T.t1s))[k]
    g.vector.quantize_mx(code[:], scale[:], tile[:, 0:512]).then_inc(s["s_qt%d" % k], 1)


def make_q(g, T):
    s = T.sem
    drain_sums(g, T, "s_yq%d", T.tq, lambda h, i: 2 * h + i, "s_pkq")
    g.vector.wait_ge(s.s_padq, 1)
    g.vector.wait_ge(s.s_pkq, 4)
    g.vector.quantize_mx(T.tqc[:], T.tqs[:], T.tq[:]).then_inc(s.s_qtq, 1)


def send_q(g, T, topo, core, c):
    s, dst = T.sem, T.cores[(c + 1) % len(T.cores)]
    m = topo.mask(core, dst)
    g.wait_ge(s.s_qtq, 1)
    return (send(g, topo, dst, m, half_c(T.wc, L2), half_c(T.tqc, 0), s.s_pair, s.s_local)
            + send(g, topo, dst, m, half_s(T.ws, L2), half_s(T.tqs, 0), s.s_pair, s.s_local))


def rank_core(g, core, r, T, topo):
    s, n = T.sem, len(T.cores)
    hs = plan(T, topo)
    free = 0 not in hs[r]
    g.scalar.dma_start(T.bbuf[:], T.b[:]).then_inc(s.s_lb, 16)
    g.sync.dma_start(T.abuf[:, 0:1024], T.a[:, 0:1024]).then_inc(s.s_la0, 16)
    g.scalar.dma_start(T.abuf[:, 1024:2048], T.a[:, 1024:2048]).then_inc(s.s_la1, 16)
    make_selection(g, T)
    g.vector.memset(T.t0[:, 256:512], 0.0).then_inc(s.s_pad, 1)
    g.vector.memset(T.t1[:, 256:768], 0.0).then_inc(s.s_pad, 1)
    if free:
        g.vector.memset(T.tq[:, 256:512], 0.0).then_inc(s.s_padq, 1)
    g.vector.wait_ge(s.s_pad, 2)
    g.vector.quantize_mx(T.wc[:, ZERO:ZERO + 128], T.ws[:, ZERO:ZERO + 128], T.t1[:, 256:768]).then_inc(s.s_qz, 1)
    g.vector.wait_ge(s.s_lb, 16)
    g.vector.quantize_mx(T.bcode[:], T.bscale[:], T.bbuf[:]).then_inc(s.s_qb, 1)
    g.tensor.wait_ge(s.s_qb, 1)
    term_chunk(g, T, 0)
    term_chunk(g, T, 1)
    quantize_selection(g, T)
    to2, q2 = T.cores[(r + 2) % n], maker(T, hs, (r + 2) % n)
    off, on = off_mask(T, topo, r), on_mask(T, topo, hs, r)
    code, scale = half_c(T.t0c, 0), half_s(T.t0s, 0)
    at, sem_c, sem_s = (L1, s.s_fwd, s.s_fwd) if q2 == to2 else (L2, s.s_fc, s.s_fs)
    out_c, out_s = [(q2, off, half_c(T.wc, at), code, sem_c)], [(q2, off, half_s(T.ws, at), scale, sem_s)]
    if not free:
        out_c.append((hs[r][0], on, half_c(T.wc, L1), code, s.s_own))
        out_s.append((hs[r][0], on, half_s(T.ws, L1), scale, s.s_own))
    g.wait_ge(s.s_qt0, 1)
    sent = fused(g, topo, out_c, s.s_local)
    sent += fused(g, topo, out_s, s.s_local)
    to = []
    for d in (1, 2, 3):
        if d in hs[r]:
            to.append((hs[r][d], off if d == 1 else on, L3, s.s_rc, s.s_rs))
        elif free:
            c = (r + d) % n
            to.append((T.cores[c], crossing(T, topo, hs, r, d)[1], slot(hs, c, d), s["s_d%d" % d], s["s_d%d" % d]))
    g.wait_ge(s.s_qt1, 1)
    sent += fused(g, topo, [(k, m, half_c(T.wc, a), half_c(T.t1c, 0), sc) for k, m, a, sc, ss in to], s.s_local)
    sent += fused(g, topo, [(k, m, half_s(T.ws, a), half_s(T.t1s, 0), ss) for k, m, a, sc, ss in to], s.s_local)
    if not free:
        a = slot(hs, (r + 2) % n, 2)
        sent += send(g, topo, to2, off, half_c(T.wc, a), half_c(T.t1c, 0), s.s_d2, s.s_local)
        sent += send(g, topo, to2, off, half_s(T.ws, a), half_s(T.t1s, 0), s.s_d2, s.s_local)
    if q2 != to2:
        sent += send(g, topo, to2, off, half_s(T.ws, L1), scale, s.s_fwd, s.s_local)
    e_far = engines(off_mask(T, topo, (r - 2) % n))
    e_fwd = e_far + (e_far if free else engines(topo.mask(hs[r][0], core) & topo.mask(hs[r][0], T.cores[(r + 1) % n])))

    def wait_term(d):
        g.tensor.wait_ge(s["s_d%d" % d], 2 * engines(crossing(T, topo, hs, (r - d) % n, d)[1]))
    first, second, third = order(hs, r)
    g.tensor.wait_ge(s.s_qe, 4)
    g.tensor.wait_ge(s.s_qt0, 1)
    unpack(g, T, 0, T.t0c, T.t0s, 0, True, False)
    g.tensor.wait_ge(s.s_qt1, 1)
    unpack(g, T, 4, T.t1c, T.t1s, 0, True, False)
    g.tensor.wait_ge(s.s_qz, 1)
    if free:
        g.tensor.wait_ge(s.s_fwd, e_fwd)
        unpack(g, T, 0, T.wc, T.ws, L1, False, True, "s_yq%d")
        make_q(g, T)
        sent += send_q(g, T, topo, core, r)
        g.tensor.wait_ge(s.s_qtq, 1)
        unpack(g, T, 0, T.t0c, T.t0s, 0, True, False)
        unpack(g, T, 0, T.wc, T.ws, L1, False, False)
        wait_term(first)
        unpack(g, T, 4, T.wc, T.ws, L3, False, False)
    else:
        wait_term(first)
        unpack(g, T, 4, T.wc, T.ws, L3, False, False)
        g.tensor.wait_ge(s.s_fwd, e_fwd)
        unpack(g, T, 0, T.wc, T.ws, L1, False, False)
    g.tensor.wait_ge(s.s_pair, 2 * engines(topo.mask(maker(T, hs, (r - 1) % n), core)))
    unpack(g, T, 0, T.wc, T.ws, L2, False, True, "s_ya%d")
    wait_term(second)
    wait_term(third)
    unpack(g, T, 4, T.wc, T.ws, L4, False, True, "s_yb%d")
    drain_sums(g, T, "s_ya%d", T.ybuf, lambda h, i: 256 * h + i, "s_yc0")
    for t in range(4):
        h, i = t // 2, t % 2
        tmp = T.ytmp[:, HALF * t:HALF * t + HALF]
        g.scalar.wait_ge(s["s_yb%d" % t], 1)
        g.scalar.activation(tmp, sums(T.acc, 4 + t, HALF, HALF), ActivationFunctionType.Copy).then_inc(s["s_cp%d" % t], 1)
        g.vector.wait_ge(s["s_cp%d" % t], 1)
        g.vector.tensor_tensor(T.ybuf[:, 256 * h + 2 + i:256 * h + 256:4], sums(T.acc, 4 + t), tmp, AluOpType.add
                               ).then_inc(s["s_yh%d" % h], 1)
    for h, queue in ((0, g.sync), (1, g.scalar)):
        queue.wait_ge(s.s_yc0, 4)
        queue.wait_ge(s["s_yh%d" % h], 2)
        queue.dma_start(T.y[:, 256 * h:256 * h + 256], T.ybuf[:, 256 * h:256 * h + 256]).then_inc(s.s_stored, 16)
    g.sync.wait_ge(s.s_stored, 32)
    g.wait_ge(s.s_local, sent)


def q_helper(g, core, r, hs, T, topo):
    s, n = T.sem, len(T.cores)
    owner = T.cores[r]
    make_selection(g, T)
    quantize_selection(g, T)
    g.vector.memset(T.tq[:, 256:512], 0.0).then_inc(s.s_padq, 1)
    e_far, e_own = engines(off_mask(T, topo, (r - 2) % n)), engines(on_mask(T, topo, hs, r))
    m = topo.mask(core, owner) & topo.mask(core, T.cores[(r + 1) % n])
    g.wait_ge(s.s_fc, e_far)
    sent = send(g, topo, owner, m, half_c(T.wc, L1), half_c(T.wc, L2), s.s_fwd, s.s_local)
    g.tensor.wait_ge(s.s_qe, 4)
    g.tensor.wait_ge(s.s_own, 2 * e_own)
    unpack(g, T, 0, T.wc, T.ws, L1, True, False)
    g.tensor.wait_ge(s.s_fc, e_far)
    g.tensor.wait_ge(s.s_fs, e_far)
    unpack(g, T, 0, T.wc, T.ws, L2, False, True, "s_yq%d")
    make_q(g, T)
    sent += send_q(g, T, topo, core, r)
    g.wait_ge(s.s_local, sent)


def relay(g, core, r, d, hs, T, topo):
    s, c = T.sem, (r + d) % len(T.cores)
    dst, a, sem = T.cores[c], slot(hs, c, d), s["s_d%d" % d]
    m, came = topo.mask(core, dst), engines(off_mask(T, topo, r) if d == 1 else on_mask(T, topo, hs, r))
    g.wait_ge(s.s_rc, came)
    sent = send(g, topo, dst, m, half_c(T.wc, a), half_c(T.wc, L3), sem, s.s_local)
    g.wait_ge(s.s_rs, came)
    sent += send(g, topo, dst, m, half_s(T.ws, a), half_s(T.ws, L3), sem, s.s_local)
    g.wait_ge(s.s_local, sent)


def rank_program(g, core, T, topo):
    r = T.rank_of(core)
    if r is not None:
        rank_core(g, core, r, T, topo)
        return
    hs = plan(T, topo)
    for k in range(len(T.cores)):
        for job, helper in hs[k].items():
            if helper == core and job == 0:
                q_helper(g, core, k, hs, T, topo)
            elif helper == core:
                relay(g, core, k, job, hs, T, topo)
